import numpy as np
import ml_dtypes


def mxq(x, axis, fmt="e4m3"):
    dtype, down = {"e4m3": (ml_dtypes.float8_e4m3fn, 7), "e5m2": (ml_dtypes.float8_e5m2, 14)}[fmt]
    v = np.moveaxis(np.asarray(x, np.float32).astype(ml_dtypes.bfloat16).astype(np.float64), axis, -1)
    blocks = v.reshape(v.shape[:-1] + (-1, 32))
    amax = np.abs(blocks).max(-1, keepdims=True)
    byte = np.maximum(np.where(amax > 0, np.frexp(amax)[1] - 1 + 127, 0) - down, 1)
    scale = np.exp2(byte - 127.0)
    codes = (blocks / scale).astype(np.float32).astype(dtype).astype(np.float64)
    return np.moveaxis((codes * scale).reshape(v.shape), -1, axis)


WIDE = False


def mx_kscale(k):
    if not WIDE:
        return np.ones(k)
    levels = np.array([10, -10, 5, -5, 0])
    if k % 512:
        return np.exp2(np.random.permutation(np.resize(levels, k // 32))).repeat(32)
    a = np.empty((k // 512, 16))
    for p in range(k // 512):
        a[p, :8] = np.random.permutation(np.resize(levels, 8))
        for g in range(8):
            far = levels[np.abs(levels - a[p, g]) >= 10]
            a[p, g + 8] = far[np.random.randint(len(far))]
    return np.exp2(a.ravel()).repeat(32)


def f64(x):
    return np.asarray(x).astype(np.float64)


def striped(idx):
    return np.tile(idx.reshape(-1, 16).T, (8, 1)).astype(np.uint16)


def unstriped(offs):
    return offs[:16].T.reshape(-1).astype(np.int64)


def striped8(idx):
    return np.concatenate([x.reshape(-1, 16).T for x in idx]).astype(np.uint16)


def runs(offs, k):
    lists = np.stack([offs[16 * r : 16 * r + 16].T.reshape(-1) for r in range(8)]).astype(np.int64)
    return lists[np.arange(k) % 512 // 64]


def pack_weight(w):
    k, n = w.shape
    w = f64(np.asarray(w, np.float32).astype(ml_dtypes.bfloat16)).reshape(k // 32, 32, n)
    amax = np.abs(w).max(1)
    byte = np.clip(np.where(amax > 0, np.frexp(amax)[1] - 1 + 127 - 7, 1), 1, 254)
    scaled = (w * np.exp2(127.0 - byte)[:, None, :]).reshape(k, n).astype(np.float32)
    words = np.ascontiguousarray(scaled.reshape(k // 512, 128, 4, n).transpose(0, 1, 3, 2)).astype(ml_dtypes.float8_e4m3fn).view(np.uint8)
    return words, np.ascontiguousarray(byte.astype(np.uint8).reshape(k // 512, 16, n))


def unpack_weight(words, scales):
    g, p, n, _ = words.shape
    vals = np.ascontiguousarray(words).view(ml_dtypes.float8_e4m3fn).astype(np.float64) * np.repeat(np.exp2(scales.astype(np.float64) - 127.0), 8, axis=1)[..., None]
    return vals.transpose(0, 1, 3, 2).reshape(g * 512, n)


K, T, S, N, H, G, U = 512, 1024, 512, 512, 512, 2048, 1024


def setup_inputs():
    n = np.random.standard_normal
    s = mx_kscale(K)[:, None]
    u = mx_kscale(S)
    packed_xT = pack_weight(n((K, T)) * s)
    packed_dT = pack_weight(n((K, G)) / s)
    return {
        "x_words": packed_xT[0],
        "x_scales": packed_xT[1],
        "w1": (n((K, H)) / np.sqrt(K) / s).astype(np.float32),
        "gs": (np.random.uniform(0.5, 1.5, (K, 1)) * s).astype(np.float32),
        "d_words": packed_dT[0],
        "d_scales": packed_dT[1],
        "mem": n((H, U)).astype(np.float32),
        "res": (1.5 * n((N, U))).astype(np.float32),
        "gn": (np.random.uniform(0.5, 1.5, (H, 1)) * u[:, None]).astype(np.float32),
        "w2": (n((H, N)) / np.sqrt(H) / u[:, None]).astype(np.float32),
        "offs": striped(np.random.permutation(T)[:S]),
        "n1": striped8(np.stack([np.random.permutation(S) for _ in range(8)])),
        "n2": striped8(np.stack([np.random.permutation(S) for _ in range(8)])),
        "n3": striped8(np.stack([np.random.permutation(S) for _ in range(8)])),
        "kidx": striped8(np.random.randint(0, G, (8, H))),
        "n4": striped8(np.stack([np.random.permutation(U)[:S] for _ in range(8)])),
    }


def reference(x_words, x_scales, w1, gs, d_words, d_scales, mem, res, gn, w2, offs, n1, n2, n3, kidx, n4):
    d_kidx = unpack_weight(d_words, d_scales)[np.arange(K)[:, None], runs(kidx, K)]
    xq = unpack_weight(x_words, x_scales)[:, unstriped(offs)]
    y = mxq(f64(w1), 0, "e4m3").T @ xq
    z = f64(gs) * (np.maximum(y, y[np.arange(H)[:, None], runs(n1, H)]) - (np.maximum(y[np.arange(H)[:, None], runs(n2, H)], y[np.arange(H)[:, None], runs(n3, H)])))
    s = 0.0625 * ((d_kidx.T @ mxq(z, 0, "e4m3")))
    nw = np.maximum(s, 0.5 * (f64(mem)[np.arange(H)[:, None], runs(n4, H)]))
    pg = f64(mem).copy()
    pg[np.arange(H)[:, None], runs(n4, H)] = nw
    z2 = f64(gn) * pg
    return f64(res) + (mxq(f64(w2), 0, "e4m3").T @ mxq(z2, 0, "e4m3"))

@@ -1,0 +1,244 @@
+from contextlib import ExitStack
+
+import concourse.mybir as mybir
+
+K, T, S, N, H, G, U = 512, 1024, 512, 512, 512, 2048, 1024
+FLOPS = 2 * (K * H * S + K * H * S + H * N * U)
+
+F32 = mybir.dt.float32
+BF16 = mybir.dt.bfloat16
+I32 = mybir.dt.int32
+U32 = mybir.dt.uint32
+U16 = mybir.dt.uint16
+U8 = mybir.dt.uint8
+FP8X4 = mybir.dt.float8_e4m3fn_x4
+ALU = mybir.AluOpType
+COPY = mybir.ActivationFunctionType.Copy
+
+P = 128
+PACK = 4
+CHUNK = 256
+
+
+def tile_picked_pqkmixpagex_none_p_kernel(
+    tc, x_words, x_scales, w1, gs, d_words, d_scales, mem, res, gn, w2, offs, n1, n2, n3, kidx, n4, out
+):
+    nc = tc.nc
+    with ExitStack() as ctx:
+        lists = ctx.enter_context(tc.tile_pool(name="lists", bufs=1))
+        keep = ctx.enter_context(tc.tile_pool(name="keep", bufs=1))
+        ring = ctx.enter_context(tc.tile_pool(name="ring", bufs=2))
+        psum = ctx.enter_context(tc.psum_pool(name="psum", bufs=1))
+
+        def sb(name, shape, dtype):
+            return keep.tile(shape, dtype, name=name, align_bytes=64)
+
+        def load_list(name, source):
+            tile = lists.tile([P, S // 16], U16, name=name)
+            nc.sync.dma_start(tile[:], source)
+            return tile
+
+        def bank(index, shape):
+            return psum.tile(shape, F32, name="bank%d" % index)
+
+        def quantize(name, source, columns):
+            codes = sb(name + "_codes", [P, columns], U32)
+            scales = sb(name + "_scales", [P, columns], U8)
+            nc.vector.quantize_mx(out=codes[:].bitcast(FP8X4), scales=scales[:], in_=source)
+            return codes, scales
+
+        def product(result, left, left_cols, right):
+            nc.tensor.matmul_mx(
+                out=result,
+                lhsT=left[0][:, left_cols].bitcast(FP8X4),
+                lhsT_scale=left[1][:, left_cols],
+                rhs=right[0][:].bitcast(FP8X4),
+                rhs_scale=right[1][:],
+                start=True,
+                stop=True,
+            )
+
+        xs_table = sb("xs_table", [P, T], U8)
+        nc.vector.memset(xs_table[:].bitcast(I32), 0)
+        ds_table = sb("ds_table", [P, G], U8)
+        nc.vector.memset(ds_table[:].bitcast(I32), 0)
+        ds_placed = sb("ds_placed", [P, H], U8)
+        nc.vector.memset(ds_placed[:].bitcast(I32), 0)
+        y = [sb("y%d" % t, [P, 2 * S], F32) for t in range(PACK)]
+        for t in range(PACK):
+            nc.vector.memset(y[t][:, S:], 0.0)
+
+        offs_t = load_list("offs_t", offs)
+        xw_table = sb("xw_table", [P, T], U32)
+        nc.sync.dma_start(xw_table[:].bitcast(I32), x_words[0].rearrange("p n r -> p (n r)").bitcast(I32))
+        xs_rows = x_scales[0].bitcast(I32)
+        for a in range(4):
+            nc.scalar.dma_start(xs_table[:].bitcast(I32)[a:P:32, :], xs_rows[a:16:4, :])
+        w1_raw = sb("w1_raw", [P, PACK, H], F32)
+        nc.sync.dma_start(w1_raw[:], w1.rearrange("(p j) c -> p j c", j=PACK))
+        n1_t = load_list("n1_t", n1)
+        n4_t = load_list("n4_t", n4)
+        mem_rows = mem.rearrange("(p t) w -> p t w", t=PACK)
+        page = [sb("page%d" % t, [P, U], F32) for t in range(PACK)]
+        nc.sync.dma_start(page[0][:], mem_rows[:, 0, :])
+        n2_t = load_list("n2_t", n2)
+        n3_t = load_list("n3_t", n3)
+        gs_t = sb("gs_t", [P, PACK], F32)
+        nc.sync.dma_start(gs_t[:], gs.rearrange("(p t) o -> p (t o)", t=PACK))
+        kidx_t = load_list("kidx_t", kidx)
+        dw_table = sb("dw_table", [P, G], U32)
+        nc.sync.dma_start(dw_table[:].bitcast(I32), d_words[0].rearrange("p n r -> p (n r)").bitcast(I32))
+        ds_rows = d_scales[0].bitcast(I32)
+        for e in range(2):
+            nc.sync.dma_start(ds_table[:].bitcast(I32)[e:P:16, :], ds_rows[e:16:2, :])
+        for t in range(1, PACK):
+            nc.sync.dma_start(page[t][:], mem_rows[:, t, :])
+        w2_raw = sb("w2_raw", [P, PACK, N], F32)
+        nc.sync.dma_start(w2_raw[:], w2.rearrange("(p j) c -> p j c", j=PACK))
+        gn_t = sb("gn_t", [P, PACK], F32)
+        nc.sync.dma_start(gn_t[:], gn.rearrange("(p t) o -> p (t o)", t=PACK))
+        res_t = sb("res_t", [P, PACK, U], F32)
+        nc.sync.dma_start(res_t[:], res.rearrange("(t p) w -> p t w", p=P))
+
+        xw = sb("xw", [P, S], U32)
+        nc.vector.tensor_copy(xw[:], xw_table[:].indirect(offs_t[:]))
+        xs = sb("xs", [P, S], U8)
+        nc.vector.tensor_copy(xs[:], xs_table[:].indirect(offs_t[:]))
+
+        w1_first = sb("w1_first", [P, P, PACK], BF16)
+        nc.vector.tensor_copy(w1_first[:], w1_raw[:].rearrange("p j (m t) -> p t m j", t=PACK)[:, 0, :, :])
+        w1_rest = sb("w1_rest", [P, PACK - 1, P, PACK], BF16)
+        nc.scalar.copy(
+            w1_rest[:].rearrange("p t m j -> p m j t"),
+            w1_raw[:].rearrange("p j (m t) -> p m j t", t=PACK)[:, :, :, 1:],
+        )
+        gs_neg = sb("gs_neg", [P, PACK], F32)
+        nc.scalar.mul(gs_neg[:], gs_t[:], -1.0)
+
+        half = [sb("half%d" % t, [P, S], F32) for t in range(PACK)]
+
+        def fetch_half(t):
+            nc.vector.tensor_scalar(half[t][:], page[t][:].indirect(n4_t[:]), 0.5, 0.0, ALU.mult, ALU.add)
+
+        def project(t):
+            source = w1_first[:] if t == 0 else w1_rest[:, t - 1, :, :]
+            w1_q = quantize("w1_%d" % t, source.rearrange("p m j -> p (m j)"), P)
+            acc = bank(t, [P, S])
+            product(acc[:], w1_q, slice(0, P), (xw, xs))
+            nc.scalar.copy(y[t][:, :S], acc[:])
+
+        project(0)
+        fetch_half(0)
+        for t in range(1, PACK):
+            project(t)
+
+        z_bf = sb("z_bf", [P, S * PACK], BF16)
+        z_planes = z_bf[:].rearrange("p (c t) -> p t c", t=PACK)
+
+        def first_pair(t):
+            got = ring.tile([P, S], F32, name="got")
+            nc.vector.tensor_copy(got[:], y[t][:].indirect(n1_t[:]))
+            return got
+
+        def larger(t, got):
+            top = ring.tile([P, S], F32, name="top")
+            nc.vector.tensor_tensor(top[:], got[:], y[t][:, :S], ALU.max)
+            return top
+
+        def keys():
+            dw_got = sb("dw_got", [P, H], U32)
+            nc.vector.tensor_copy(dw_got[:], dw_table[:].indirect(kidx_t[:]))
+            ds_got = sb("ds_got", [P, H], U8)
+            nc.vector.tensor_copy(ds_got[:], ds_table[:].indirect(kidx_t[:]))
+            dw = sb("dw", [P, H], U32)
+            nc.vector.tensor_copy(
+                dw[:].rearrange("p (t m) -> p m t", t=PACK), dw_got[:].rearrange("p (m t) -> p m t", t=PACK)
+            )
+            ds_dealt = sb("ds_dealt", [P, H], U8)
+            nc.vector.tensor_copy(
+                ds_dealt[:].rearrange("p (t m) -> p m t", t=PACK), ds_got[:].rearrange("p (m t) -> p m t", t=PACK)
+            )
+            for a in range(4):
+                start = 16 * (a // 2) + a % 2
+                nc.sync.dma_start(ds_placed[:].bitcast(I32)[a:P:32, :], ds_dealt[:].bitcast(I32)[start:P:32, :])
+            return dw, ds_placed
+
+        got = first_pair(0)
+        top = larger(0, got)
+        for t in range(PACK):
+            if t + 1 < PACK:
+                got = first_pair(t + 1)
+            d2 = ring.tile([P, S], F32, name="d2")
+            nc.vector.tensor_tensor(d2[:], y[t][:].indirect(n2_t[:]), top[:], ALU.subtract)
+            d3 = ring.tile([P, S], F32, name="d3")
+            nc.vector.tensor_tensor(d3[:], y[t][:].indirect(n3_t[:]), top[:], ALU.subtract)
+            if t + 1 < PACK:
+                top = larger(t + 1, got)
+            else:
+                fetch_half(1)
+            gap = ring.tile([P, S], F32, name="gap")
+            nc.vector.tensor_tensor(gap[:], d2[:], d3[:], ALU.max)
+            nc.scalar.activation(z_planes[:, t, :], gap[:], COPY, scale=gs_neg[:, t : t + 1])
+            if t == 1:
+                d_q = keys()
+
+        w2_bf = sb("w2_bf", [P, N, PACK], BF16)
+        nc.scalar.copy(
+            w2_bf[:].rearrange("p (c i) j -> p c j i", i=4), w2_raw[:].rearrange("p j (c i) -> p c j i", i=4)
+        )
+        fetch_half(2)
+        w2_q = quantize("w2", w2_bf[:].rearrange("p c j -> p (c j)"), N)
+        z_q = quantize("z", z_bf[:], S)
+        fetch_half(3)
+
+        scores = []
+        for t in range(PACK):
+            acc = bank(PACK + t, [P, S])
+            product(acc[:], d_q, slice(t * P, (t + 1) * P), z_q)
+            scores.append(acc)
+
+        new = [sb("new%d" % t, [P, S], F32) for t in range(PACK)]
+
+        def choose(t):
+            nc.vector.scalar_tensor_tensor(new[t][:], scores[t][:], 0.0625, half[t][:], ALU.mult, ALU.max)
+
+        z2_bf = sb("z2_bf", [P, U * PACK], BF16)
+        z2_planes = z2_bf[:].rearrange("p (c t) -> p t c", t=PACK)
+        choose(0)
+        for t in range(PACK):
+            if t + 1 < PACK:
+                choose(t + 1)
+            nc.vector.tensor_copy(page[t][:].indirect(n4_t[:]), new[t][:])
+            if t + 1 < PACK:
+                nc.scalar.activation(z2_planes[:, t, :], page[t][:], COPY, scale=gn_t[:, t : t + 1])
+
+        out_rows = out.rearrange("(t p) w -> p t w", p=P)
+        last = PACK - 1
+        chunks = U // CHUNK
+
+        def prepare(c):
+            cols = slice(c * CHUNK, (c + 1) * CHUNK)
+            nc.scalar.activation(z2_planes[:, last, cols], page[last][:, cols], COPY, scale=gn_t[:, last : last + 1])
+            z2_q = quantize("z2_%d" % c, z2_bf[:, c * CHUNK * PACK : (c + 1) * CHUNK * PACK], CHUNK)
+            accs = []
+            for pair in range(2):
+                acc = bank((2 * c + pair) % 8, [P, 2, CHUNK])
+                for u in range(2):
+                    t = 2 * pair + u
+                    product(acc[:, u, :], w2_q, slice(t * P, (t + 1) * P), z2_q)
+                accs.append(acc)
+            return accs
+
+        def finish(c, accs):
+            cols = slice(c * CHUNK, (c + 1) * CHUNK)
+            for pair in range(2):
+                rows = slice(2 * pair, 2 * pair + 2)
+                total = sb("total%d_%d" % (c, pair), [P, 2, CHUNK], F32)
+                nc.vector.tensor_tensor(total[:], accs[pair][:], res_t[:, rows, cols], ALU.add)
+                nc.sync.dma_start(out_rows[:, rows, cols], total[:])
+
+        pending = prepare(0)
+        for c in range(chunks):
+            following = prepare(c + 1) if c + 1 < chunks else None
+            finish(c, pending)
+            pending = following

@@ -17,7 +17,7 @@ COPY = mybir.ActivationFunctionType.Copy
 
 P = 128
 PACK = 4
-CHUNK = 256
+WIDTHS = (128, 128, 256, 512)
 
 
 def tile_picked_pqkmixpagex_none_p_kernel(
@@ -59,38 +59,34 @@ def tile_picked_pqkmixpagex_none_p_kernel(
             )
 
         xs_table = sb("xs_table", [P, T], U8)
-        nc.vector.memset(xs_table[:].bitcast(I32), 0)
+        nc.gpsimd.memset(xs_table[:].bitcast(I32), 0)
         ds_table = sb("ds_table", [P, G], U8)
         nc.vector.memset(ds_table[:].bitcast(I32), 0)
         ds_placed = sb("ds_placed", [P, H], U8)
-        nc.vector.memset(ds_placed[:].bitcast(I32), 0)
+        nc.gpsimd.memset(ds_placed[:].bitcast(I32), 0)
         y = [sb("y%d" % t, [P, 2 * S], F32) for t in range(PACK)]
-        for t in range(PACK):
-            nc.vector.memset(y[t][:, S:], 0.0)
 
         offs_t = load_list("offs_t", offs)
-        xw_table = sb("xw_table", [P, T], U32)
-        nc.sync.dma_start(xw_table[:].bitcast(I32), x_words[0].rearrange("p n r -> p (n r)").bitcast(I32))
+        kidx_t = load_list("kidx_t", kidx)
         xs_rows = x_scales[0].bitcast(I32)
         for a in range(4):
-            nc.scalar.dma_start(xs_table[:].bitcast(I32)[a:P:32, :], xs_rows[a:16:4, :])
+            nc.sync.dma_start(xs_table[:].bitcast(I32)[a:P:32, :], xs_rows[a:16:4, :])
+        nc.sync.dma_start(ds_table[:].bitcast(I32)[0:P:8, :], d_scales[0].bitcast(I32))
+        xw_table = sb("xw_table", [P, T], U32)
+        nc.sync.dma_start(xw_table[:].bitcast(I32), x_words[0].rearrange("p n r -> p (n r)").bitcast(I32))
         w1_raw = sb("w1_raw", [P, PACK, H], F32)
         nc.sync.dma_start(w1_raw[:], w1.rearrange("(p j) c -> p j c", j=PACK))
-        n1_t = load_list("n1_t", n1)
         n4_t = load_list("n4_t", n4)
         mem_rows = mem.rearrange("(p t) w -> p t w", t=PACK)
         page = [sb("page%d" % t, [P, U], F32) for t in range(PACK)]
         nc.sync.dma_start(page[0][:], mem_rows[:, 0, :])
+        n1_t = load_list("n1_t", n1)
         n2_t = load_list("n2_t", n2)
         n3_t = load_list("n3_t", n3)
         gs_t = sb("gs_t", [P, PACK], F32)
         nc.sync.dma_start(gs_t[:], gs.rearrange("(p t) o -> p (t o)", t=PACK))
-        kidx_t = load_list("kidx_t", kidx)
         dw_table = sb("dw_table", [P, G], U32)
         nc.sync.dma_start(dw_table[:].bitcast(I32), d_words[0].rearrange("p n r -> p (n r)").bitcast(I32))
-        ds_rows = d_scales[0].bitcast(I32)
-        for e in range(2):
-            nc.sync.dma_start(ds_table[:].bitcast(I32)[e:P:16, :], ds_rows[e:16:2, :])
         for t in range(1, PACK):
             nc.sync.dma_start(page[t][:], mem_rows[:, t, :])
         w2_raw = sb("w2_raw", [P, PACK, N], F32)
@@ -100,10 +96,12 @@ def tile_picked_pqkmixpagex_none_p_kernel(
         res_t = sb("res_t", [P, PACK, U], F32)
         nc.sync.dma_start(res_t[:], res.rearrange("(t p) w -> p t w", p=P))
 
-        xw = sb("xw", [P, S], U32)
-        nc.vector.tensor_copy(xw[:], xw_table[:].indirect(offs_t[:]))
         xs = sb("xs", [P, S], U8)
         nc.vector.tensor_copy(xs[:], xs_table[:].indirect(offs_t[:]))
+        xw = sb("xw", [P, S], U32)
+        nc.vector.tensor_copy(xw[:], xw_table[:].indirect(offs_t[:]))
+        ds_got = sb("ds_got", [P, H], U8)
+        nc.vector.tensor_copy(ds_got[:], ds_table[:].indirect(kidx_t[:]))
 
         w1_first = sb("w1_first", [P, P, PACK], BF16)
         nc.vector.tensor_copy(w1_first[:], w1_raw[:].rearrange("p j (m t) -> p t m j", t=PACK)[:, 0, :, :])
@@ -113,24 +111,30 @@ def tile_picked_pqkmixpagex_none_p_kernel(
             w1_raw[:].rearrange("p j (m t) -> p m j t", t=PACK)[:, :, :, 1:],
         )
         gs_neg = sb("gs_neg", [P, PACK], F32)
-        nc.scalar.mul(gs_neg[:], gs_t[:], -1.0)
+        nc.gpsimd.tensor_scalar(gs_neg[:], gs_t[:], -1.0, 0.0, ALU.mult, ALU.add)
 
-        half = [sb("half%d" % t, [P, S], F32) for t in range(PACK)]
+        def project(first, count, source):
+            w1_q = quantize("w1_%d" % first, source, count * P)
+            for u in range(count):
+                acc = bank(first + u, [P, S])
+                product(acc[:], w1_q, slice(u * P, (u + 1) * P), (xw, xs))
+                nc.scalar.copy(y[first + u][:, :S], acc[:])
 
-        def fetch_half(t):
-            nc.vector.tensor_scalar(half[t][:], page[t][:].indirect(n4_t[:]), 0.5, 0.0, ALU.mult, ALU.add)
+        def fetch_half(t, tile):
+            nc.vector.tensor_scalar(tile[:], page[t][:].indirect(n4_t[:]), 0.5, 0.0, ALU.mult, ALU.add)
+            return tile
 
-        def project(t):
-            source = w1_first[:] if t == 0 else w1_rest[:, t - 1, :, :]
-            w1_q = quantize("w1_%d" % t, source.rearrange("p m j -> p (m j)"), P)
-            acc = bank(t, [P, S])
-            product(acc[:], w1_q, slice(0, P), (xw, xs))
-            nc.scalar.copy(y[t][:, :S], acc[:])
-
-        project(0)
-        fetch_half(0)
-        for t in range(1, PACK):
-            project(t)
+        project(0, 1, w1_first[:].rearrange("p m j -> p (m j)"))
+        ds_dealt = sb("w1_first", [P, H], U8)
+        nc.vector.tensor_copy(
+            ds_dealt[:].rearrange("p (t m) -> p m t", t=PACK), ds_got[:].rearrange("p (m t) -> p m t", t=PACK)
+        )
+        half = [fetch_half(0, sb("ds_got", [P, S], F32))]
+        project(1, 1, w1_rest[:, 0, :, :].rearrange("p m j -> p (m j)"))
+        project(2, 2, w1_rest[:, 1:, :, :].rearrange("p t m j -> p (t m j)"))
+        for a in range(4):
+            start = 8 * a
+            nc.sync.dma_start(ds_placed[:].bitcast(I32)[a:P:32, :], ds_dealt[:].bitcast(I32)[start:P:32, :])
 
         z_bf = sb("z_bf", [P, S * PACK], BF16)
         z_planes = z_bf[:].rearrange("p (c t) -> p t c", t=PACK)
@@ -145,29 +149,15 @@ def tile_picked_pqkmixpagex_none_p_kernel(
             nc.vector.tensor_tensor(top[:], got[:], y[t][:, :S], ALU.max)
             return top
 
-        def keys():
-            dw_got = sb("dw_got", [P, H], U32)
-            nc.vector.tensor_copy(dw_got[:], dw_table[:].indirect(kidx_t[:]))
-            ds_got = sb("ds_got", [P, H], U8)
-            nc.vector.tensor_copy(ds_got[:], ds_table[:].indirect(kidx_t[:]))
-            dw = sb("dw", [P, H], U32)
-            nc.vector.tensor_copy(
-                dw[:].rearrange("p (t m) -> p m t", t=PACK), dw_got[:].rearrange("p (m t) -> p m t", t=PACK)
-            )
-            ds_dealt = sb("ds_dealt", [P, H], U8)
-            nc.vector.tensor_copy(
-                ds_dealt[:].rearrange("p (t m) -> p m t", t=PACK), ds_got[:].rearrange("p (m t) -> p m t", t=PACK)
-            )
-            for a in range(4):
-                start = 16 * (a // 2) + a % 2
-                nc.sync.dma_start(ds_placed[:].bitcast(I32)[a:P:32, :], ds_dealt[:].bitcast(I32)[start:P:32, :])
-            return dw, ds_placed
-
+        dw_got = sb("dw_got", [P, H], U32)
+        dw = sb("dw", [P, H], U32)
         got = first_pair(0)
         top = larger(0, got)
         for t in range(PACK):
             if t + 1 < PACK:
                 got = first_pair(t + 1)
+            else:
+                nc.vector.tensor_copy(dw_got[:], dw_table[:].indirect(kidx_t[:]))
             d2 = ring.tile([P, S], F32, name="d2")
             nc.vector.tensor_tensor(d2[:], y[t][:].indirect(n2_t[:]), top[:], ALU.subtract)
             d3 = ring.tile([P, S], F32, name="d3")
@@ -175,21 +165,22 @@ def tile_picked_pqkmixpagex_none_p_kernel(
             if t + 1 < PACK:
                 top = larger(t + 1, got)
             else:
-                fetch_half(1)
+                nc.vector.tensor_copy(
+                    dw[:].rearrange("p (t m) -> p m t", t=PACK), dw_got[:].rearrange("p (m t) -> p m t", t=PACK)
+                )
             gap = ring.tile([P, S], F32, name="gap")
             nc.vector.tensor_tensor(gap[:], d2[:], d3[:], ALU.max)
             nc.scalar.activation(z_planes[:, t, :], gap[:], COPY, scale=gs_neg[:, t : t + 1])
-            if t == 1:
-                d_q = keys()
+        d_q = (dw, ds_placed)
 
         w2_bf = sb("w2_bf", [P, N, PACK], BF16)
         nc.scalar.copy(
             w2_bf[:].rearrange("p (c i) j -> p c j i", i=4), w2_raw[:].rearrange("p j (c i) -> p c j i", i=4)
         )
-        fetch_half(2)
-        w2_q = quantize("w2", w2_bf[:].rearrange("p c j -> p (c j)"), N)
+        half.append(fetch_half(1, ring.tile([P, S], F32, name="d3")))
+        half.append(fetch_half(2, ring.tile([P, S], F32, name="top")))
         z_q = quantize("z", z_bf[:], S)
-        fetch_half(3)
+        half.append(fetch_half(3, sb("z_bf", [P, S], F32)))
 
         scores = []
         for t in range(PACK):
@@ -212,33 +203,47 @@ def tile_picked_pqkmixpagex_none_p_kernel(
             if t + 1 < PACK:
                 nc.scalar.activation(z2_planes[:, t, :], page[t][:], COPY, scale=gn_t[:, t : t + 1])
 
+        w2_codes = sb("new2", [P, N], U32)
+        w2_scales = sb("w2_scales", [P, N], U8)
+        nc.vector.quantize_mx(
+            out=w2_codes[:].bitcast(FP8X4), scales=w2_scales[:], in_=w2_bf[:].rearrange("p c j -> p (c j)")
+        )
+        w2_q = (w2_codes, w2_scales)
+
         out_rows = out.rearrange("(t p) w -> p t w", p=P)
         last = PACK - 1
-        chunks = U // CHUNK
+        banks_used = []
 
-        def prepare(c):
-            cols = slice(c * CHUNK, (c + 1) * CHUNK)
+        def prepare(first, width):
+            cols = slice(first, first + width)
             nc.scalar.activation(z2_planes[:, last, cols], page[last][:, cols], COPY, scale=gn_t[:, last : last + 1])
-            z2_q = quantize("z2_%d" % c, z2_bf[:, c * CHUNK * PACK : (c + 1) * CHUNK * PACK], CHUNK)
-            accs = []
-            for pair in range(2):
-                acc = bank((2 * c + pair) % 8, [P, 2, CHUNK])
-                for u in range(2):
-                    t = 2 * pair + u
+            z2_q = quantize("z2_%d" % first, z2_bf[:, first * PACK : (first + width) * PACK], width)
+            per_bank = 512 // width
+            jobs = []
+            for t0 in range(0, PACK, per_bank):
+                acc = bank(len(banks_used) % 8, [P, per_bank, width])
+                banks_used.append(acc)
+                for u in range(per_bank):
+                    t = t0 + u
                     product(acc[:, u, :], w2_q, slice(t * P, (t + 1) * P), z2_q)
-                accs.append(acc)
-            return accs
+                jobs.append((acc, slice(t0, t0 + per_bank), cols))
+            return jobs
 
-        def finish(c, accs):
-            cols = slice(c * CHUNK, (c + 1) * CHUNK)
-            for pair in range(2):
-                rows = slice(2 * pair, 2 * pair + 2)
-                total = sb("total%d_%d" % (c, pair), [P, 2, CHUNK], F32)
-                nc.vector.tensor_tensor(total[:], accs[pair][:], res_t[:, rows, cols], ALU.add)
-                nc.sync.dma_start(out_rows[:, rows, cols], total[:])
+        def finish(job):
+            acc, rows, cols = job
+            total = sb("total%d_%d" % (rows.start, cols.start), [P, rows.stop - rows.start, cols.stop - cols.start], F32)
+            nc.vector.tensor_tensor(total[:], acc[:], res_t[:, rows, cols], ALU.add)
+            nc.sync.dma_start(out_rows[:, rows, cols], total[:])
 
-        pending = prepare(0)
-        for c in range(chunks):
-            following = prepare(c + 1) if c + 1 < chunks else None
-            finish(c, pending)
-            pending = following
+        waiting = []
+        first = 0
+        for width in WIDTHS:
+            jobs = prepare(first, width)
+            first += width
+            for job in waiting:
+                finish(job)
+            waiting = jobs[-1:]
+            for job in jobs[:-1]:
+                finish(job)
+        for job in waiting:
+            finish(job)

from contextlib import ExitStack

import concourse.mybir as mybir

K, T, S, N, H, G, U = 512, 1024, 512, 512, 512, 2048, 1024
FLOPS = 2 * (K * H * S + K * H * S + H * N * U)

F32 = mybir.dt.float32
BF16 = mybir.dt.bfloat16
I32 = mybir.dt.int32
U32 = mybir.dt.uint32
U16 = mybir.dt.uint16
U8 = mybir.dt.uint8
FP8X4 = mybir.dt.float8_e4m3fn_x4
ALU = mybir.AluOpType
COPY = mybir.ActivationFunctionType.Copy

P = 128
PACK = 4
WIDTHS = (128, 128, 256, 512)


def tile_picked_pqkmixpagex_none_p_kernel(
    tc, x_words, x_scales, w1, gs, d_words, d_scales, mem, res, gn, w2, offs, n1, n2, n3, kidx, n4, out
):
    nc = tc.nc
    with ExitStack() as ctx:
        lists = ctx.enter_context(tc.tile_pool(name="lists", bufs=1))
        keep = ctx.enter_context(tc.tile_pool(name="keep", bufs=1))
        ring = ctx.enter_context(tc.tile_pool(name="ring", bufs=2))
        psum = ctx.enter_context(tc.psum_pool(name="psum", bufs=1))

        def sb(name, shape, dtype):
            return keep.tile(shape, dtype, name=name, align_bytes=64)

        def load_list(name, source):
            tile = lists.tile([P, S // 16], U16, name=name)
            nc.sync.dma_start(tile[:], source)
            return tile

        def bank(index, shape):
            return psum.tile(shape, F32, name="bank%d" % index)

        def quantize(name, source, columns):
            codes = sb(name + "_codes", [P, columns], U32)
            scales = sb(name + "_scales", [P, columns], U8)
            nc.vector.quantize_mx(out=codes[:].bitcast(FP8X4), scales=scales[:], in_=source)
            return codes, scales

        def product(result, left, left_cols, right):
            nc.tensor.matmul_mx(
                out=result,
                lhsT=left[0][:, left_cols].bitcast(FP8X4),
                lhsT_scale=left[1][:, left_cols],
                rhs=right[0][:].bitcast(FP8X4),
                rhs_scale=right[1][:],
                start=True,
                stop=True,
            )

        xs_table = sb("xs_table", [P, T], U8)
        nc.gpsimd.memset(xs_table[:].bitcast(I32), 0)
        ds_table = sb("ds_table", [P, G], U8)
        nc.vector.memset(ds_table[:].bitcast(I32), 0)
        ds_placed = sb("ds_placed", [P, H], U8)
        nc.gpsimd.memset(ds_placed[:].bitcast(I32), 0)
        y = [sb("y%d" % t, [P, 2 * S], F32) for t in range(PACK)]

        offs_t = load_list("offs_t", offs)
        kidx_t = load_list("kidx_t", kidx)
        xs_rows = x_scales[0].bitcast(I32)
        for a in range(4):
            nc.sync.dma_start(xs_table[:].bitcast(I32)[a:P:32, :], xs_rows[a:16:4, :])
        nc.sync.dma_start(ds_table[:].bitcast(I32)[0:P:8, :], d_scales[0].bitcast(I32))
        xw_table = sb("xw_table", [P, T], U32)
        nc.sync.dma_start(xw_table[:].bitcast(I32), x_words[0].rearrange("p n r -> p (n r)").bitcast(I32))
        w1_raw = sb("w1_raw", [P, PACK, H], F32)
        nc.sync.dma_start(w1_raw[:], w1.rearrange("(p j) c -> p j c", j=PACK))
        n4_t = load_list("n4_t", n4)
        mem_rows = mem.rearrange("(p t) w -> p t w", t=PACK)
        page = [sb("page%d" % t, [P, U], F32) for t in range(PACK)]
        nc.sync.dma_start(page[0][:], mem_rows[:, 0, :])
        n1_t = load_list("n1_t", n1)
        n2_t = load_list("n2_t", n2)
        n3_t = load_list("n3_t", n3)
        gs_t = sb("gs_t", [P, PACK], F32)
        nc.sync.dma_start(gs_t[:], gs.rearrange("(p t) o -> p (t o)", t=PACK))
        dw_table = sb("dw_table", [P, G], U32)
        nc.sync.dma_start(dw_table[:].bitcast(I32), d_words[0].rearrange("p n r -> p (n r)").bitcast(I32))
        for t in range(1, PACK):
            nc.sync.dma_start(page[t][:], mem_rows[:, t, :])
        w2_raw = sb("w2_raw", [P, PACK, N], F32)
        nc.sync.dma_start(w2_raw[:], w2.rearrange("(p j) c -> p j c", j=PACK))
        gn_t = sb("gn_t", [P, PACK], F32)
        nc.sync.dma_start(gn_t[:], gn.rearrange("(p t) o -> p (t o)", t=PACK))
        res_t = sb("res_t", [P, PACK, U], F32)
        nc.sync.dma_start(res_t[:], res.rearrange("(t p) w -> p t w", p=P))

        xs = sb("xs", [P, S], U8)
        nc.vector.tensor_copy(xs[:], xs_table[:].indirect(offs_t[:]))
        xw = sb("xw", [P, S], U32)
        nc.vector.tensor_copy(xw[:], xw_table[:].indirect(offs_t[:]))
        ds_got = sb("ds_got", [P, H], U8)
        nc.vector.tensor_copy(ds_got[:], ds_table[:].indirect(kidx_t[:]))

        w1_first = sb("w1_first", [P, P, PACK], BF16)
        nc.vector.tensor_copy(w1_first[:], w1_raw[:].rearrange("p j (m t) -> p t m j", t=PACK)[:, 0, :, :])
        w1_rest = sb("w1_rest", [P, PACK - 1, P, PACK], BF16)
        nc.scalar.copy(
            w1_rest[:].rearrange("p t m j -> p m j t"),
            w1_raw[:].rearrange("p j (m t) -> p m j t", t=PACK)[:, :, :, 1:],
        )
        gs_neg = sb("gs_neg", [P, PACK], F32)
        nc.gpsimd.tensor_scalar(gs_neg[:], gs_t[:], -1.0, 0.0, ALU.mult, ALU.add)

        def project(first, count, source):
            w1_q = quantize("w1_%d" % first, source, count * P)
            for u in range(count):
                acc = bank(first + u, [P, S])
                product(acc[:], w1_q, slice(u * P, (u + 1) * P), (xw, xs))
                nc.scalar.copy(y[first + u][:, :S], acc[:])

        def fetch_half(t, tile):
            nc.vector.tensor_scalar(tile[:], page[t][:].indirect(n4_t[:]), 0.5, 0.0, ALU.mult, ALU.add)
            return tile

        project(0, 1, w1_first[:].rearrange("p m j -> p (m j)"))
        ds_dealt = sb("w1_first", [P, H], U8)
        nc.vector.tensor_copy(
            ds_dealt[:].rearrange("p (t m) -> p m t", t=PACK), ds_got[:].rearrange("p (m t) -> p m t", t=PACK)
        )
        half = [fetch_half(0, sb("ds_got", [P, S], F32))]
        project(1, 1, w1_rest[:, 0, :, :].rearrange("p m j -> p (m j)"))
        project(2, 2, w1_rest[:, 1:, :, :].rearrange("p t m j -> p (t m j)"))
        for a in range(4):
            start = 8 * a
            nc.sync.dma_start(ds_placed[:].bitcast(I32)[a:P:32, :], ds_dealt[:].bitcast(I32)[start:P:32, :])

        z_bf = sb("z_bf", [P, S * PACK], BF16)
        z_planes = z_bf[:].rearrange("p (c t) -> p t c", t=PACK)

        def first_pair(t):
            got = ring.tile([P, S], F32, name="got")
            nc.vector.tensor_copy(got[:], y[t][:].indirect(n1_t[:]))
            return got

        def larger(t, got):
            top = ring.tile([P, S], F32, name="top")
            nc.vector.tensor_tensor(top[:], got[:], y[t][:, :S], ALU.max)
            return top

        dw_got = sb("dw_got", [P, H], U32)
        dw = sb("dw", [P, H], U32)
        got = first_pair(0)
        top = larger(0, got)
        for t in range(PACK):
            if t + 1 < PACK:
                got = first_pair(t + 1)
            else:
                nc.vector.tensor_copy(dw_got[:], dw_table[:].indirect(kidx_t[:]))
            d2 = ring.tile([P, S], F32, name="d2")
            nc.vector.tensor_tensor(d2[:], y[t][:].indirect(n2_t[:]), top[:], ALU.subtract)
            d3 = ring.tile([P, S], F32, name="d3")
            nc.vector.tensor_tensor(d3[:], y[t][:].indirect(n3_t[:]), top[:], ALU.subtract)
            if t + 1 < PACK:
                top = larger(t + 1, got)
            else:
                nc.vector.tensor_copy(
                    dw[:].rearrange("p (t m) -> p m t", t=PACK), dw_got[:].rearrange("p (m t) -> p m t", t=PACK)
                )
            gap = ring.tile([P, S], F32, name="gap")
            nc.vector.tensor_tensor(gap[:], d2[:], d3[:], ALU.max)
            nc.scalar.activation(z_planes[:, t, :], gap[:], COPY, scale=gs_neg[:, t : t + 1])
        d_q = (dw, ds_placed)

        w2_bf = sb("w2_bf", [P, N, PACK], BF16)
        nc.scalar.copy(
            w2_bf[:].rearrange("p (c i) j -> p c j i", i=4), w2_raw[:].rearrange("p j (c i) -> p c j i", i=4)
        )
        half.append(fetch_half(1, ring.tile([P, S], F32, name="d3")))
        half.append(fetch_half(2, ring.tile([P, S], F32, name="top")))
        z_q = quantize("z", z_bf[:], S)
        half.append(fetch_half(3, sb("z_bf", [P, S], F32)))

        scores = []
        for t in range(PACK):
            acc = bank(PACK + t, [P, S])
            product(acc[:], d_q, slice(t * P, (t + 1) * P), z_q)
            scores.append(acc)

        new = [sb("new%d" % t, [P, S], F32) for t in range(PACK)]

        def choose(t):
            nc.vector.scalar_tensor_tensor(new[t][:], scores[t][:], 0.0625, half[t][:], ALU.mult, ALU.max)

        z2_bf = sb("z2_bf", [P, U * PACK], BF16)
        z2_planes = z2_bf[:].rearrange("p (c t) -> p t c", t=PACK)
        choose(0)
        for t in range(PACK):
            if t + 1 < PACK:
                choose(t + 1)
            nc.vector.tensor_copy(page[t][:].indirect(n4_t[:]), new[t][:])
            if t + 1 < PACK:
                nc.scalar.activation(z2_planes[:, t, :], page[t][:], COPY, scale=gn_t[:, t : t + 1])

        w2_codes = sb("new2", [P, N], U32)
        w2_scales = sb("w2_scales", [P, N], U8)
        nc.vector.quantize_mx(
            out=w2_codes[:].bitcast(FP8X4), scales=w2_scales[:], in_=w2_bf[:].rearrange("p c j -> p (c j)")
        )
        w2_q = (w2_codes, w2_scales)

        out_rows = out.rearrange("(t p) w -> p t w", p=P)
        last = PACK - 1
        banks_used = []

        def prepare(first, width):
            cols = slice(first, first + width)
            nc.scalar.activation(z2_planes[:, last, cols], page[last][:, cols], COPY, scale=gn_t[:, last : last + 1])
            z2_q = quantize("z2_%d" % first, z2_bf[:, first * PACK : (first + width) * PACK], width)
            per_bank = 512 // width
            jobs = []
            for t0 in range(0, PACK, per_bank):
                acc = bank(len(banks_used) % 8, [P, per_bank, width])
                banks_used.append(acc)
                for u in range(per_bank):
                    t = t0 + u
                    product(acc[:, u, :], w2_q, slice(t * P, (t + 1) * P), z2_q)
                jobs.append((acc, slice(t0, t0 + per_bank), cols))
            return jobs

        def finish(job):
            acc, rows, cols = job
            total = sb("total%d_%d" % (rows.start, cols.start), [P, rows.stop - rows.start, cols.stop - cols.start], F32)
            nc.vector.tensor_tensor(total[:], acc[:], res_t[:, rows, cols], ALU.add)
            nc.sync.dma_start(out_rows[:, rows, cols], total[:])

        waiting = []
        first = 0
        for width in WIDTHS:
            jobs = prepare(first, width)
            first += width
            for job in waiting:
                finish(job)
            waiting = jobs[-1:]
            for job in jobs[:-1]:
                finish(job)
        for job in waiting:
            finish(job)
